import numpy as np
import ml_dtypes


def mxq(x, axis, fmt="e4m3"):
    dtype, down = {"e4m3": (ml_dtypes.float8_e4m3fn, 7), "e5m2": (ml_dtypes.float8_e5m2, 14)}[fmt]
    v = np.moveaxis(np.asarray(x, np.float32).astype(ml_dtypes.bfloat16).astype(np.float64), axis, -1)
    blocks = v.reshape(v.shape[:-1] + (-1, 32))
    amax = np.abs(blocks).max(-1, keepdims=True)
    byte = np.maximum(np.where(amax > 0, np.frexp(amax)[1] - 1 + 127, 0) - down, 1)
    scale = np.exp2(byte - 127.0)
    codes = (blocks / scale).astype(np.float32).astype(dtype).astype(np.float64)
    return np.moveaxis((codes * scale).reshape(v.shape), -1, axis)


WIDE = False


def mx_kscale(k):
    if not WIDE:
        return np.ones(k)
    levels = np.array([10, -10, 5, -5, 0])
    if k % 512:
        return np.exp2(np.random.permutation(np.resize(levels, k // 32))).repeat(32)
    a = np.empty((k // 512, 16))
    for p in range(k // 512):
        a[p, :8] = np.random.permutation(np.resize(levels, 8))
        for g in range(8):
            far = levels[np.abs(levels - a[p, g]) >= 10]
            a[p, g + 8] = far[np.random.randint(len(far))]
    return np.exp2(a.ravel()).repeat(32)


def f64(x):
    return np.asarray(x).astype(np.float64)


def striped(idx):
    return np.tile(idx.reshape(-1, 16).T, (8, 1)).astype(np.uint16)


def unstriped(offs):
    return offs[:16].T.reshape(-1).astype(np.int64)


E2M1 = np.array([0.0, 0.5, 1.0, 1.5, 2.0, 3.0, 4.0, 6.0, -0.0, -0.5, -1.0, -1.5, -2.0, -3.0, -4.0, -6.0])


def pack_weight(w, fmt):
    k, n = w.shape
    w = f64(np.asarray(w, np.float32).astype(ml_dtypes.bfloat16)).reshape(k // 32, 32, n)
    amax = np.abs(w).max(1)
    if fmt == "e4m3":
        byte = np.frexp(amax)[1] - 1 + 127 - 7
    else:
        mant, ex = np.frexp(amax / 6.0)
        byte = np.where(mant > 0.5, ex, ex - 1) + 127
    byte = np.clip(np.where(amax > 0, byte, 1), 1, 254)
    scaled = (w * np.exp2(127.0 - byte)[:, None, :]).reshape(k, n).astype(np.float32)
    by_word = np.ascontiguousarray(scaled.reshape(k // 512, 128, 4, n).transpose(0, 1, 3, 2))
    if fmt == "e4m3":
        words = by_word.astype(ml_dtypes.float8_e4m3fn).view(np.uint8)
    else:
        c = by_word.astype(ml_dtypes.float4_e2m1fn).view(np.uint8) & 0xF
        words = (c[..., 0::2] | (c[..., 1::2] << 4)).reshape(k // 512, 128, 2 * n)
    return np.ascontiguousarray(words), np.ascontiguousarray(byte.astype(np.uint8).reshape(k // 512, 16, n))


def unpack_weight(words, scales, fmt):
    g, _, n = scales.shape
    words = np.ascontiguousarray(words).reshape(g, 128, n, -1)
    if fmt == "e4m3":
        vals = words.view(ml_dtypes.float8_e4m3fn).astype(np.float64)
    else:
        nib = np.empty((g, 128, n, 4), np.uint8)
        nib[..., 0::2] = words & 0xF
        nib[..., 1::2] = words >> 4
        vals = E2M1[nib]
    vals = vals * np.repeat(np.exp2(scales.astype(np.float64) - 127.0), 8, axis=1)[..., None]
    return vals.transpose(0, 1, 3, 2).reshape(g * 512, n)


def gelu(v):
    return 0.5 * v * (1.0 + np.tanh(np.sqrt(2.0 / np.pi) * (v + 0.044715 * v**3)))


def twice(P):
    return np.random.permutation(np.repeat(np.arange(P), 2))


K, T, S, P, H = 1024, 4096, 1024, 512, 1024

def setup_inputs():
    n = np.random.standard_normal
    s = mx_kscale(K)[:, None]
    u = mx_kscale(H)[:, None]
    d = {}
    d["tab_words"], d["tab_scales"] = pack_weight(n((K, T)) * s, "e4m3")
    d["offs"] = striped(np.random.permutation(T)[:S])
    d["w1"] = (n((K, H)) / s * u.T / K ** 0.5).astype(np.float32)
    d["w2_words"], d["w2_scales"] = pack_weight(n((K, H)) / s / u.T / K ** 0.5, "e2m1")
    d["pos1"] = striped(np.random.permutation(S)[:P])
    d["pos2"] = striped(np.random.permutation(S)[:P])
    d["w3"] = (0.6 * n((H, H)) / u / H ** 0.5).astype(np.float32)
    d["pos3"] = striped(twice(P))
    d["hs"] = (np.exp(0.3 * n(H)) / u[:, 0]).astype(np.float32)
    return d

def reference(tab_words, tab_scales, offs, w1, w2_words, w2_scales, pos1, pos2, w3, pos3, hs):
    v = unpack_weight(tab_words, tab_scales, "e4m3")[:, unstriped(offs)]
    w2 = unpack_weight(w2_words, w2_scales, "e2m1")
    a = mxq(f64(w1), 0, "e4m3").T @ v
    b = w2.T @ v
    h = np.square(a) * b - a
    low = np.minimum(h[:, unstriped(pos1)], h[:, unstriped(pos2)])
    y = mxq(f64(w3), 0, "e4m3").T @ mxq(low, 0, "e4m3")
    damp = np.exp(-np.abs(y[:, unstriped(pos3)]))
    out = damp * (f64(hs)[:, None] * h)
    return out

@@ -1,0 +1,256 @@
+from contextlib import ExitStack
+
+import concourse.mybir as mybir
+
+K, T, S, C, H = 1024, 4096, 1024, 512, 1024
+FLOPS = 2 * (2 * K * H * S) + 2 * H * H * C
+
+F32 = mybir.dt.float32
+BF16 = mybir.dt.bfloat16
+I32 = mybir.dt.int32
+U32 = mybir.dt.uint32
+U16 = mybir.dt.uint16
+U8 = mybir.dt.uint8
+FP8X4 = mybir.dt.float8_e4m3fn_x4
+FP4X4 = mybir.dt.float4_e2m1fn_x4
+ACT = mybir.ActivationFunctionType
+ALU = mybir.AluOpType
+
+P = 128
+PACK = 4
+PASS = P * PACK
+BANK = 512
+LIST_ROWS = 16
+
+
+def tile_list_contest_log_features_kernel(
+    tc, tab_words, tab_scales, offs, w1, w2_words, w2_scales, pos1, pos2, w3, pos3, hs, out
+):
+    nc = tc.nc
+    passes = K // PASS
+    groups = H // PASS
+    row_tiles = [(b, t) for b in range(groups) for t in range(PACK)]
+
+    with ExitStack() as ctx:
+        keep = ctx.enter_context(tc.tile_pool(name="keep", bufs=1))
+        wide = ctx.enter_context(tc.tile_pool(name="wide", bufs=2))
+        raw = ctx.enter_context(tc.tile_pool(name="raw", bufs=4))
+        work = ctx.enter_context(tc.tile_pool(name="work", bufs=3))
+        psum = ctx.enter_context(tc.psum_pool(name="psum", bufs=8))
+
+        def load_list(name, src, entries):
+            lst = keep.tile([P, entries // LIST_ROWS], U16, name=name)
+            nc.sync.dma_start(lst[:], src)
+            return lst
+
+        def load_scale_rows(queue, dst, src):
+            for q in range(4):
+                queue.dma_start(
+                    dst[32 * q : 32 * q + 4, :, :].bitcast(I32),
+                    src[:, 4 * q : 4 * q + 4, :].rearrange("a r n -> r a n").bitcast(I32),
+                )
+
+        def load_weight_block(w, a, b):
+            block = raw.tile([P, PACK, PASS], F32, name="w_raw")
+            rows = w[a * PASS : (a + 1) * PASS, b * PASS : (b + 1) * PASS]
+            nc.sync.dma_start(block[:], rows.rearrange("(p j) c -> p j c", j=PACK))
+            return block
+
+        def round_weight_block(block):
+            rounded = work.tile([P, PASS * PACK], BF16, name="w_bf16", align_bytes=64)
+            nc.scalar.activation(
+                out=rounded[:].rearrange("p (t m j) -> p m j t", t=PACK, j=PACK),
+                in_=block[:].rearrange("p j (m t) -> p m j t", t=PACK),
+                func=ACT.Copy,
+            )
+            return rounded
+
+        def quantise(name, rounded):
+            codes = keep.tile([P, PASS], U32, name=name + "_codes", align_bytes=64)
+            scales = keep.tile([P, PASS], U8, name=name + "_scales", align_bytes=64)
+            nc.vector.quantize_mx(out=codes[:].bitcast(FP8X4), scales=scales[:], in_=rounded[:])
+            return codes, scales
+
+        table_scales = keep.tile([P, passes, T], U8, name="table_scales")
+        nc.vector.memset(table_scales[:].rearrange("p a n -> p (a n)").bitcast(I32), 0)
+        w2_scale_rows = keep.tile([P, passes, H], U8, name="w2_scale_rows")
+        nc.gpsimd.memset(w2_scale_rows[:].rearrange("p a n -> p (a n)").bitcast(I32), 0)
+
+        entry_list = load_list("entry_list", offs, S)
+        side_lists = [load_list("side1_list", pos1, C), load_list("side2_list", pos2, C)]
+        contact_list = load_list("contact_list", pos3, S)
+        row_scale = keep.tile([P, groups, PACK], F32, name="row_scale")
+        nc.sync.dma_start(row_scale[:], hs.rearrange("(b p t) -> p b t", b=groups, t=PACK))
+        w2_raw = keep.tile([P, passes, 2 * H], U8, name="w2_raw")
+        for a in range(passes):
+            nc.sync.dma_start(w2_raw[:, a, :].bitcast(I32), w2_words[a].bitcast(I32))
+        w1_raw = {(0, 0): load_weight_block(w1, 0, 0)}
+        load_scale_rows(nc.sync, table_scales, tab_scales)
+        load_scale_rows(nc.sync, w2_scale_rows, w2_scales)
+
+        def load_table(a):
+            words = wide.tile([P, T], I32, name="table_words", tag="wide")
+            nc.sync.dma_start(words[:], tab_words[a].rearrange("p n i -> p (n i)").bitcast(I32))
+            return words
+
+        w1_raw[1, 0] = load_weight_block(w1, 1, 0)
+        table = [load_table(a) for a in range(passes)]
+        for a in range(passes):
+            w1_raw[a, 1] = load_weight_block(w1, a, 1)
+
+        w2_codes = keep.tile([P, passes * groups, PACK, 2 * P], U8, name="w2_codes", align_bytes=64)
+        nc.vector.tensor_copy(
+            w2_codes[:].bitcast(U16),
+            w2_raw[:].bitcast(U16).rearrange("p a (b m t) -> p (a b) t m", b=groups, t=PACK),
+        )
+
+        v_codes = keep.tile([P, passes, S], U32, name="v_codes", align_bytes=64)
+        v_scales = keep.tile([P, passes, S], U8, name="v_scales", align_bytes=64)
+        for a in range(passes):
+            nc.vector.tensor_copy(v_scales[:, a, :], table_scales[:, a, :].indirect(entry_list[:]))
+        w2_planes = keep.tile([P, passes * groups, PACK, P], U8, name="w2_planes", align_bytes=64)
+        nc.vector.tensor_copy(
+            w2_planes[:], w2_scale_rows[:].rearrange("p a (b m t) -> p (a b) t m", b=groups, t=PACK)
+        )
+        w1_mx = {}
+        for a in range(passes):
+            w1_mx[a, 0] = quantise("w1_%d0" % a, round_weight_block(w1_raw[a, 0]))
+        nc.vector.tensor_copy(v_codes[:, 0, :], table[0][:].bitcast(U32).indirect(entry_list[:]))
+        cols = BANK // LIST_ROWS
+        for u in range(S // BANK):
+            nc.vector.tensor_copy(
+                v_codes[:, 1, u * BANK : (u + 1) * BANK],
+                table[1][:].bitcast(U32).indirect(entry_list[:, u * cols : (u + 1) * cols]),
+            )
+
+        h = [keep.tile([P, S], F32, name="h%d" % i) for i in range(len(row_tiles))]
+        picked = {}
+        low_mx = {}
+        w3_mx = {}
+
+        def products(i, u):
+            b, t = row_tiles[i]
+            entries = slice(u * BANK, (u + 1) * BANK)
+            rows = slice(t * P, (t + 1) * P)
+            first = psum.tile([P, BANK], F32, name="acc", tag="acc")
+            for a in range(passes):
+                codes, scales = w1_mx[a, b]
+                nc.tensor.matmul_mx(
+                    out=first[:], lhsT=codes[:, rows].bitcast(FP8X4), lhsT_scale=scales[:, rows],
+                    rhs=v_codes[:, a, entries].bitcast(FP8X4), rhs_scale=v_scales[:, a, entries],
+                    start=(a == 0), stop=(a == passes - 1),
+                )
+            second = psum.tile([P, BANK], F32, name="acc", tag="acc")
+            for a in range(passes):
+                nc.tensor.matmul_mx(
+                    out=second[:], lhsT=w2_codes[:, a * groups + b, t, :].bitcast(FP4X4),
+                    lhsT_scale=w2_planes[:, a * groups + b, t, :],
+                    rhs=v_codes[:, a, entries].bitcast(FP8X4), rhs_scale=v_scales[:, a, entries],
+                    start=(a == 0), stop=(a == passes - 1),
+                )
+            squared = work.tile([P, BANK], F32, name="squared")
+            nc.scalar.activation(out=squared[:], in_=first[:], func=ACT.Square)
+            cubic = work.tile([P, BANK], F32, name="cubic")
+            nc.vector.tensor_tensor(cubic[:], second[:], squared[:], ALU.mult)
+            return first, cubic
+
+        def difference(i, u, first, cubic):
+            nc.vector.tensor_tensor(h[i][:, u * BANK : (u + 1) * BANK], cubic[:], first[:], ALU.subtract)
+
+        def pick_side(i, side):
+            b, t = row_tiles[i]
+            if b not in picked:
+                picked[b] = wide.tile([P, 2, PACK, C], F32, name="picked", tag="wide")
+            nc.vector.tensor_copy(picked[b][:, side, t, :], h[i][:].indirect(side_lists[side][:]))
+
+        def smaller_side(b):
+            low = work.tile([P, C * PACK], BF16, name="low", align_bytes=64, bufs=2)
+            nc.vector.tensor_tensor(
+                low[:].rearrange("p (c i t) -> p c t i", i=4, t=PACK),
+                picked[b][:, 0, :, :].rearrange("p t (c i) -> p c t i", i=4),
+                picked[b][:, 1, :, :].rearrange("p t (c i) -> p c t i", i=4),
+                ALU.min,
+            )
+            return low
+
+        later_blocks = [("w1", a, 1) for a in range(passes)] + [("w3", a, b) for b in range(groups) for a in range(groups)]
+        pending = None
+        for i in range(len(row_tiles)):
+            made = [products(i, 0)]
+            if i > 0:
+                pick_side(i - 1, 0)
+            made.append(products(i, 1))
+            difference(i, 0, *made[0])
+            if i > 0:
+                pick_side(i - 1, 1)
+            difference(i, 1, *made[1])
+            if pending is not None:
+                name, a, b, rounded = pending
+                (w1_mx if name == "w1" else w3_mx)[a, b] = quantise("%s_%d%d" % (name, a, b), rounded)
+                pending = None
+            if i < len(later_blocks):
+                name, a, b = later_blocks[i]
+                block = w1_raw[a, b] if name == "w1" else load_weight_block(w3, a, b)
+                pending = (name, a, b, round_weight_block(block))
+            if i == PACK:
+                low_first = smaller_side(0)
+            if i == PACK + 1:
+                low_mx[0] = quantise("low0", low_first)
+        last = len(row_tiles) - 1
+        pick_side(last, 0)
+        pick_side(last, 1)
+        low_mx[1] = quantise("low1", smaller_side(1))
+
+        y = keep.tile([P, len(row_tiles) * C], F32, name="y")
+
+        def second_stage(i):
+            b, t = row_tiles[i]
+            rows = slice(t * P, (t + 1) * P)
+            acc = psum.tile([P, C], F32, name="acc", tag="acc")
+            for a in range(groups):
+                codes, scales = w3_mx[a, b]
+                nc.tensor.matmul_mx(
+                    out=acc[:], lhsT=codes[:, rows].bitcast(FP8X4), lhsT_scale=scales[:, rows],
+                    rhs=low_mx[a][0][:].bitcast(FP8X4), rhs_scale=low_mx[a][1][:],
+                    start=(a == 0), stop=(a == groups - 1),
+                )
+            start = (last - i) * C
+            nc.scalar.copy(y[:, start : start + C], acc[:])
+
+        def damp(i, lo, hi):
+            start = (last - i) * C
+            width = C * min(i + 1, 3)
+            fetched = work.tile([P, hi - lo], F32, name="fetched", bufs=4)
+            nc.vector.tensor_copy(
+                fetched[:], y[:, start : start + width].indirect(contact_list[:, lo // LIST_ROWS : hi // LIST_ROWS])
+            )
+            nc.scalar.activation(out=fetched[:], in_=fetched[:], func=ACT.Abs)
+            nc.scalar.activation(out=fetched[:], in_=fetched[:], func=ACT.Exp, scale=-1.0)
+            return fetched
+
+        out_rows = out.rearrange("(b p t) j -> b t p j", b=groups, t=PACK)
+
+        def finish(i, lo, hi, damping):
+            b, t = row_tiles[i]
+            nc.vector.scalar_tensor_tensor(
+                out=h[i][:, lo:hi], in0=h[i][:, lo:hi], scalar=row_scale[:, b, t : t + 1], in1=damping[:],
+                op0=ALU.mult, op1=ALU.mult,
+            )
+            nc.sync.dma_start(out_rows[b, t][:, lo:hi], h[i][:, lo:hi])
+
+        steps = []
+        for i in range(len(row_tiles)):
+            piece = S // 4 if i in (0, last) else (S // 2 if i in (1, last - 1) else S)
+            steps.extend((i, lo, lo + piece) for lo in range(0, S, piece))
+        for i in range(2):
+            second_stage(i)
+        waiting = []
+        for i, lo, hi in steps:
+            if lo == 0 and 0 < i < last:
+                second_stage(i + 1)
+            waiting.append((i, lo, hi, damp(i, lo, hi)))
+            if len(waiting) > 2:
+                finish(*waiting[0])
+                waiting = waiting[1:]
+        for step in waiting:
+            finish(*step)

@@ -21,6 +21,10 @@ PACK = 4
 PASS = P * PACK
 BANK = 512
 LIST_ROWS = 16
+NV = 1
+EV = (0,)
+MB = 2
+FV = (6, 7)
 
 
 def tile_list_contest_log_features_kernel(
@@ -51,7 +55,7 @@ def tile_list_contest_log_features_kernel(
                 )
 
         def load_weight_block(w, a, b):
-            block = raw.tile([P, PACK, PASS], F32, name="w_raw")
+            block = raw.tile([P, PACK, PASS], F32, name="w_raw", tag="w_raw")
             rows = w[a * PASS : (a + 1) * PASS, b * PASS : (b + 1) * PASS]
             nc.sync.dma_start(block[:], rows.rearrange("(p j) c -> p j c", j=PACK))
             return block
@@ -148,20 +152,28 @@ def tile_list_contest_log_features_kernel(
                     rhs=v_codes[:, a, entries].bitcast(FP8X4), rhs_scale=v_scales[:, a, entries],
                     start=(a == 0), stop=(a == passes - 1),
                 )
-            squared = work.tile([P, BANK], F32, name="squared")
-            nc.scalar.activation(out=squared[:], in_=first[:], func=ACT.Square)
+            if i == 0:
+                squared = work.tile([P, BANK], F32, name="squared", bufs=2)[:]
+            else:
+                squared = picked_slice(i - 1, u)
+            nc.scalar.activation(out=squared, in_=first[:], func=ACT.Square)
             cubic = work.tile([P, BANK], F32, name="cubic")
-            nc.vector.tensor_tensor(cubic[:], second[:], squared[:], ALU.mult)
-            return first, cubic
+            nc.vector.tensor_tensor(cubic[:], second[:], squared, ALU.mult)
+            if i < NV:
+                nc.vector.tensor_tensor(h[i][:, entries], cubic[:], first[:], ALU.subtract)
+            else:
+                linear = work.tile([P, BANK], F32, name="linear")
+                nc.scalar.copy(linear[:], first[:])
+                nc.gpsimd.tensor_tensor(h[i][:, entries], cubic[:], linear[:], ALU.subtract)
 
-        def difference(i, u, first, cubic):
-            nc.vector.tensor_tensor(h[i][:, u * BANK : (u + 1) * BANK], cubic[:], first[:], ALU.subtract)
-
-        def pick_side(i, side):
+        def picked_slice(i, side):
             b, t = row_tiles[i]
             if b not in picked:
                 picked[b] = wide.tile([P, 2, PACK, C], F32, name="picked", tag="wide")
-            nc.vector.tensor_copy(picked[b][:, side, t, :], h[i][:].indirect(side_lists[side][:]))
+            return picked[b][:, side, t, :]
+
+        def pick_side(i, side):
+            nc.vector.tensor_copy(picked_slice(i, side), h[i][:].indirect(side_lists[side][:]))
 
         def smaller_side(b):
             low = work.tile([P, C * PACK], BF16, name="low", align_bytes=64, bufs=2)
@@ -176,14 +188,10 @@ def tile_list_contest_log_features_kernel(
         later_blocks = [("w1", a, 1) for a in range(passes)] + [("w3", a, b) for b in range(groups) for a in range(groups)]
         pending = None
         for i in range(len(row_tiles)):
-            made = [products(i, 0)]
-            if i > 0:
-                pick_side(i - 1, 0)
-            made.append(products(i, 1))
-            difference(i, 0, *made[0])
-            if i > 0:
-                pick_side(i - 1, 1)
-            difference(i, 1, *made[1])
+            for u in range(S // BANK):
+                products(i, u)
+                if i > 0:
+                    pick_side(i - 1, u)
             if pending is not None:
                 name, a, b, rounded = pending
                 (w1_mx if name == "w1" else w3_mx)[a, b] = quantise("%s_%d%d" % (name, a, b), rounded)
@@ -200,6 +208,8 @@ def tile_list_contest_log_features_kernel(
         pick_side(last, 0)
         pick_side(last, 1)
         low_mx[1] = quantise("low1", smaller_side(1))
+        for i, (b, t) in enumerate(row_tiles):
+            nc.scalar.activation(out=h[i][:], in_=h[i][:], func=ACT.Copy, scale=row_scale[:, b, t : t + 1])
 
         y = keep.tile([P, len(row_tiles) * C], F32, name="y")
 
@@ -215,27 +225,33 @@ def tile_list_contest_log_features_kernel(
                     start=(a == 0), stop=(a == groups - 1),
                 )
             start = (last - i) * C
-            nc.scalar.copy(y[:, start : start + C], acc[:])
+            if i in EV:
+                nc.vector.tensor_copy(y[:, start : start + C], acc[:])
+            else:
+                nc.scalar.copy(y[:, start : start + C], acc[:])
+
+        fetched_pairs = {}
 
         def damp(i, lo, hi):
             start = (last - i) * C
             width = C * min(i + 1, 3)
-            fetched = work.tile([P, hi - lo], F32, name="fetched", bufs=4)
+            if i // 2 not in fetched_pairs:
+                fetched_pairs[i // 2] = raw.tile([P, 2, S], F32, name="fetched", tag="w_raw")
+            fetched = fetched_pairs[i // 2][:, i % 2, lo:hi]
             nc.vector.tensor_copy(
-                fetched[:], y[:, start : start + width].indirect(contact_list[:, lo // LIST_ROWS : hi // LIST_ROWS])
+                fetched, y[:, start : start + width].indirect(contact_list[:, lo // LIST_ROWS : hi // LIST_ROWS])
             )
-            nc.scalar.activation(out=fetched[:], in_=fetched[:], func=ACT.Abs)
-            nc.scalar.activation(out=fetched[:], in_=fetched[:], func=ACT.Exp, scale=-1.0)
+            magnitude = work.tile([P, hi - lo], F32, name="magnitude", bufs=MB)
+            nc.scalar.activation(out=magnitude[:], in_=fetched, func=ACT.Abs)
+            nc.scalar.activation(out=fetched, in_=magnitude[:], func=ACT.Exp, scale=-1.0)
             return fetched
 
         out_rows = out.rearrange("(b p t) j -> b t p j", b=groups, t=PACK)
 
         def finish(i, lo, hi, damping):
             b, t = row_tiles[i]
-            nc.vector.scalar_tensor_tensor(
-                out=h[i][:, lo:hi], in0=h[i][:, lo:hi], scalar=row_scale[:, b, t : t + 1], in1=damping[:],
-                op0=ALU.mult, op1=ALU.mult,
-            )
+            engine = nc.vector if i in FV else nc.gpsimd
+            engine.tensor_tensor(h[i][:, lo:hi], h[i][:, lo:hi], damping, ALU.mult)
             nc.sync.dma_start(out_rows[b, t][:, lo:hi], h[i][:, lo:hi])
 
         steps = []

@@ -21,8 +21,17 @@ PACK = 4
 PASS = P * PACK
 BANK = 512
 LIST_ROWS = 16
-NV = 1
-EV = (0,)
+NV = 2
+RING = 3
+SPARE = 32
+GP = (512, 512, 512, 512, 512, 512, 512, 256)
+SP = ((512, 512), (512, 512), (512, 512), (512, 512), (512, 512), (512, 512), (512, 512), (512, 256, 256))
+LATE = True
+YB = 2
+HS = (2, 3, 4, 5)
+HG = (0, 1)
+CASTS = (0, 1, 3, 4, 6, 7)
+EV = (4, 5, 6, 7)
 MB = 2
 FV = (6, 7)
 
@@ -38,7 +47,7 @@ def tile_list_contest_log_features_kernel(
     with ExitStack() as ctx:
         keep = ctx.enter_context(tc.tile_pool(name="keep", bufs=1))
         wide = ctx.enter_context(tc.tile_pool(name="wide", bufs=2))
-        raw = ctx.enter_context(tc.tile_pool(name="raw", bufs=4))
+        raw = ctx.enter_context(tc.tile_pool(name="raw", bufs=2))
         work = ctx.enter_context(tc.tile_pool(name="work", bufs=3))
         psum = ctx.enter_context(tc.psum_pool(name="psum", bufs=8))
 
@@ -63,8 +72,8 @@ def tile_list_contest_log_features_kernel(
         def round_weight_block(block):
             rounded = work.tile([P, PASS * PACK], BF16, name="w_bf16", align_bytes=64)
             nc.scalar.activation(
-                out=rounded[:].rearrange("p (t m j) -> p m j t", t=PACK, j=PACK),
-                in_=block[:].rearrange("p j (m t) -> p m j t", t=PACK),
+                out=rounded[:].rearrange("p (t m j) -> p m t j", t=PACK, j=PACK),
+                in_=block[:].rearrange("p j (m t) -> p m t j", t=PACK),
                 func=ACT.Copy,
             )
             return rounded
@@ -75,8 +84,10 @@ def tile_list_contest_log_features_kernel(
             nc.vector.quantize_mx(out=codes[:].bitcast(FP8X4), scales=scales[:], in_=rounded[:])
             return codes, scales
 
-        table_scales = keep.tile([P, passes, T], U8, name="table_scales")
-        nc.vector.memset(table_scales[:].rearrange("p a n -> p (a n)").bitcast(I32), 0)
+        table_scales = keep.tile([P, T], U8, name="table_scales")
+        nc.vector.memset(table_scales[:].bitcast(I32), 0)
+        v_scales = [keep.tile([P, S], U8, name="v_scales%d" % a, align_bytes=64) for a in range(passes)]
+        nc.gpsimd.memset(v_scales[1][:].bitcast(I32), 0)
         w2_scale_rows = keep.tile([P, passes, H], U8, name="w2_scale_rows")
         nc.gpsimd.memset(w2_scale_rows[:].rearrange("p a n -> p (a n)").bitcast(I32), 0)
 
@@ -89,7 +100,10 @@ def tile_list_contest_log_features_kernel(
         for a in range(passes):
             nc.sync.dma_start(w2_raw[:, a, :].bitcast(I32), w2_words[a].bitcast(I32))
         w1_raw = {(0, 0): load_weight_block(w1, 0, 0)}
-        load_scale_rows(nc.sync, table_scales, tab_scales)
+        for q in range(4):
+            nc.sync.dma_start(
+                table_scales[32 * q : 32 * q + 8, :].bitcast(I32), tab_scales[:, 4 * q : 4 * q + 4, :].bitcast(I32)
+            )
         load_scale_rows(nc.sync, w2_scale_rows, w2_scales)
 
         def load_table(a):
@@ -99,8 +113,6 @@ def tile_list_contest_log_features_kernel(
 
         w1_raw[1, 0] = load_weight_block(w1, 1, 0)
         table = [load_table(a) for a in range(passes)]
-        for a in range(passes):
-            w1_raw[a, 1] = load_weight_block(w1, a, 1)
 
         w2_codes = keep.tile([P, passes * groups, PACK, 2 * P], U8, name="w2_codes", align_bytes=64)
         nc.vector.tensor_copy(
@@ -109,9 +121,8 @@ def tile_list_contest_log_features_kernel(
         )
 
         v_codes = keep.tile([P, passes, S], U32, name="v_codes", align_bytes=64)
-        v_scales = keep.tile([P, passes, S], U8, name="v_scales", align_bytes=64)
-        for a in range(passes):
-            nc.vector.tensor_copy(v_scales[:, a, :], table_scales[:, a, :].indirect(entry_list[:]))
+        nc.vector.tensor_copy(v_scales[0][:], table_scales[:].indirect(entry_list[:]))
+        nc.sync.dma_start(v_scales[1][0:112, :].bitcast(I32), v_scales[0][4:116, :].bitcast(I32))
         w2_planes = keep.tile([P, passes * groups, PACK, P], U8, name="w2_planes", align_bytes=64)
         nc.vector.tensor_copy(
             w2_planes[:], w2_scale_rows[:].rearrange("p a (b m t) -> p (a b) t m", b=groups, t=PACK)
@@ -141,7 +152,7 @@ def tile_list_contest_log_features_kernel(
                 codes, scales = w1_mx[a, b]
                 nc.tensor.matmul_mx(
                     out=first[:], lhsT=codes[:, rows].bitcast(FP8X4), lhsT_scale=scales[:, rows],
-                    rhs=v_codes[:, a, entries].bitcast(FP8X4), rhs_scale=v_scales[:, a, entries],
+                    rhs=v_codes[:, a, entries].bitcast(FP8X4), rhs_scale=v_scales[a][:, entries],
                     start=(a == 0), stop=(a == passes - 1),
                 )
             second = psum.tile([P, BANK], F32, name="acc", tag="acc")
@@ -149,7 +160,7 @@ def tile_list_contest_log_features_kernel(
                 nc.tensor.matmul_mx(
                     out=second[:], lhsT=w2_codes[:, a * groups + b, t, :].bitcast(FP4X4),
                     lhsT_scale=w2_planes[:, a * groups + b, t, :],
-                    rhs=v_codes[:, a, entries].bitcast(FP8X4), rhs_scale=v_scales[:, a, entries],
+                    rhs=v_codes[:, a, entries].bitcast(FP8X4), rhs_scale=v_scales[a][:, entries],
                     start=(a == 0), stop=(a == passes - 1),
                 )
             if i == 0:
@@ -176,7 +187,7 @@ def tile_list_contest_log_features_kernel(
             nc.vector.tensor_copy(picked_slice(i, side), h[i][:].indirect(side_lists[side][:]))
 
         def smaller_side(b):
-            low = work.tile([P, C * PACK], BF16, name="low", align_bytes=64, bufs=2)
+            low = work.tile([P, C * PACK], BF16, name="low", tag="low", align_bytes=64, bufs=1)
             nc.vector.tensor_tensor(
                 low[:].rearrange("p (c i t) -> p c t i", i=4, t=PACK),
                 picked[b][:, 0, :, :].rearrange("p t (c i) -> p c t i", i=4),
@@ -187,6 +198,7 @@ def tile_list_contest_log_features_kernel(
 
         later_blocks = [("w1", a, 1) for a in range(passes)] + [("w3", a, b) for b in range(groups) for a in range(groups)]
         pending = None
+        late = []
         for i in range(len(row_tiles)):
             for u in range(S // BANK):
                 products(i, u)
@@ -196,10 +208,13 @@ def tile_list_contest_log_features_kernel(
                 name, a, b, rounded = pending
                 (w1_mx if name == "w1" else w3_mx)[a, b] = quantise("%s_%d%d" % (name, a, b), rounded)
                 pending = None
-            if i < len(later_blocks):
-                name, a, b = later_blocks[i]
-                block = w1_raw[a, b] if name == "w1" else load_weight_block(w3, a, b)
-                pending = (name, a, b, round_weight_block(block))
+            if i in CASTS:
+                name, a, b = later_blocks[CASTS.index(i)]
+                block = load_weight_block(w1 if name == "w1" else w3, a, b)
+                if LATE and name == "w3" and b == 1:
+                    late.append((a, round_weight_block(block)))
+                else:
+                    pending = (name, a, b, round_weight_block(block))
             if i == PACK:
                 low_first = smaller_side(0)
             if i == PACK + 1:
@@ -207,11 +222,26 @@ def tile_list_contest_log_features_kernel(
         last = len(row_tiles) - 1
         pick_side(last, 0)
         pick_side(last, 1)
+        if pending is not None:
+            name, a, b, rounded = pending
+            w3_mx[a, b] = quantise("%s_%d%d" % (name, a, b), rounded)
         low_mx[1] = quantise("low1", smaller_side(1))
-        for i, (b, t) in enumerate(row_tiles):
+        if LATE:
+            late_codes = work.tile([P, groups, PASS], U32, name="late_codes", tag="low", align_bytes=64, bufs=1)
+            for a, rounded in late:
+                scales = keep.tile([P, PASS], U8, name="late_scales%d" % a, align_bytes=64)
+                nc.vector.quantize_mx(out=late_codes[:, a, :].bitcast(FP8X4), scales=scales[:], in_=rounded[:])
+                w3_mx[a, 1] = (late_codes[:, a, :], scales)
+        for i in HS:
+            b, t = row_tiles[i]
             nc.scalar.activation(out=h[i][:], in_=h[i][:], func=ACT.Copy, scale=row_scale[:, b, t : t + 1])
+        for i in HG:
+            b, t = row_tiles[i]
+            nc.gpsimd.tensor_scalar(h[i][:], h[i][:], row_scale[:, b, t : t + 1], 0.0, ALU.mult, ALU.add)
 
-        y = keep.tile([P, len(row_tiles) * C], F32, name="y")
+        y = [keep.tile([P, C + SPARE], F32, name="y%d" % r) for r in range(RING)]
+        for r in range(RING):
+            nc.gpsimd.memset(y[r][:, C:], 0.0)
 
         def second_stage(i):
             b, t = row_tiles[i]
@@ -224,23 +254,29 @@ def tile_list_contest_log_features_kernel(
                     rhs=low_mx[a][0][:].bitcast(FP8X4), rhs_scale=low_mx[a][1][:],
                     start=(a == 0), stop=(a == groups - 1),
                 )
-            start = (last - i) * C
             if i in EV:
-                nc.vector.tensor_copy(y[:, start : start + C], acc[:])
+                nc.vector.tensor_copy(y[i % RING][:, :C], acc[:])
             else:
-                nc.scalar.copy(y[:, start : start + C], acc[:])
+                nc.scalar.copy(y[i % RING][:, :C], acc[:])
 
-        fetched_pairs = {}
+        fetched_groups = {}
+
+        def fetched_slice(i, lo, hi):
+            b, t = row_tiles[i]
+            if b not in fetched_groups:
+                fetched_groups[b] = wide.tile([P, PACK, S], F32, name="fetched", tag="wide")
+            return fetched_groups[b][:, t, lo:hi]
+
+        def fetch(i):
+            for lo in range(0, S, GP[i]):
+                hi = lo + GP[i]
+                nc.vector.tensor_copy(
+                    fetched_slice(i, lo, hi),
+                    y[i % RING][:].indirect(contact_list[:, lo // LIST_ROWS : hi // LIST_ROWS]),
+                )
 
         def damp(i, lo, hi):
-            start = (last - i) * C
-            width = C * min(i + 1, 3)
-            if i // 2 not in fetched_pairs:
-                fetched_pairs[i // 2] = raw.tile([P, 2, S], F32, name="fetched", tag="w_raw")
-            fetched = fetched_pairs[i // 2][:, i % 2, lo:hi]
-            nc.vector.tensor_copy(
-                fetched, y[:, start : start + width].indirect(contact_list[:, lo // LIST_ROWS : hi // LIST_ROWS])
-            )
+            fetched = fetched_slice(i, lo, hi)
             magnitude = work.tile([P, hi - lo], F32, name="magnitude", bufs=MB)
             nc.scalar.activation(out=magnitude[:], in_=fetched, func=ACT.Abs)
             nc.scalar.activation(out=fetched, in_=magnitude[:], func=ACT.Exp, scale=-1.0)
@@ -250,22 +286,29 @@ def tile_list_contest_log_features_kernel(
 
         def finish(i, lo, hi, damping):
             b, t = row_tiles[i]
-            engine = nc.vector if i in FV else nc.gpsimd
-            engine.tensor_tensor(h[i][:, lo:hi], h[i][:, lo:hi], damping, ALU.mult)
+            if i in FV:
+                nc.vector.scalar_tensor_tensor(
+                    out=h[i][:, lo:hi], in0=h[i][:, lo:hi], scalar=row_scale[:, b, t : t + 1], in1=damping,
+                    op0=ALU.mult, op1=ALU.mult,
+                )
+            else:
+                if i not in HS and i not in HG:
+                    nc.gpsimd.tensor_scalar(damping, damping, row_scale[:, b, t : t + 1], 0.0, ALU.mult, ALU.add)
+                nc.gpsimd.tensor_tensor(h[i][:, lo:hi], h[i][:, lo:hi], damping, ALU.mult)
             nc.sync.dma_start(out_rows[b, t][:, lo:hi], h[i][:, lo:hi])
 
-        steps = []
-        for i in range(len(row_tiles)):
-            piece = S // 4 if i in (0, last) else (S // 2 if i in (1, last - 1) else S)
-            steps.extend((i, lo, lo + piece) for lo in range(0, S, piece))
-        for i in range(2):
+        for i in range(RING):
             second_stage(i)
         waiting = []
-        for i, lo, hi in steps:
-            if lo == 0 and 0 < i < last:
-                second_stage(i + 1)
-            waiting.append((i, lo, hi, damp(i, lo, hi)))
-            if len(waiting) > 2:
+        for i in range(len(row_tiles)):
+            fetch(i)
+            if i + RING <= last:
+                second_stage(i + RING)
+            lo = 0
+            for width in SP[i]:
+                waiting.append((i, lo, lo + width, damp(i, lo, lo + width)))
+                lo = lo + width
+            while len(waiting) > 0 and waiting[0][0] < i:
                 finish(*waiting[0])
                 waiting = waiting[1:]
         for step in waiting:

from contextlib import ExitStack

import concourse.mybir as mybir

K, T, S, C, H = 1024, 4096, 1024, 512, 1024
FLOPS = 2 * (2 * K * H * S) + 2 * H * H * C

F32 = mybir.dt.float32
BF16 = mybir.dt.bfloat16
I32 = mybir.dt.int32
U32 = mybir.dt.uint32
U16 = mybir.dt.uint16
U8 = mybir.dt.uint8
FP8X4 = mybir.dt.float8_e4m3fn_x4
FP4X4 = mybir.dt.float4_e2m1fn_x4
ACT = mybir.ActivationFunctionType
ALU = mybir.AluOpType

P = 128
PACK = 4
PASS = P * PACK
BANK = 512
LIST_ROWS = 16
NV = 2
RING = 3
SPARE = 32
GP = (512, 512, 512, 512, 512, 512, 512, 256)
SP = ((512, 512), (512, 512), (512, 512), (512, 512), (512, 512), (512, 512), (512, 512), (512, 256, 256))
LATE = True
YB = 2
HS = (2, 3, 4, 5)
HG = (0, 1)
CASTS = (0, 1, 3, 4, 6, 7)
EV = (4, 5, 6, 7)
MB = 2
FV = (6, 7)


def tile_list_contest_log_features_kernel(
    tc, tab_words, tab_scales, offs, w1, w2_words, w2_scales, pos1, pos2, w3, pos3, hs, out
):
    nc = tc.nc
    passes = K // PASS
    groups = H // PASS
    row_tiles = [(b, t) for b in range(groups) for t in range(PACK)]

    with ExitStack() as ctx:
        keep = ctx.enter_context(tc.tile_pool(name="keep", bufs=1))
        wide = ctx.enter_context(tc.tile_pool(name="wide", bufs=2))
        raw = ctx.enter_context(tc.tile_pool(name="raw", bufs=2))
        work = ctx.enter_context(tc.tile_pool(name="work", bufs=3))
        psum = ctx.enter_context(tc.psum_pool(name="psum", bufs=8))

        def load_list(name, src, entries):
            lst = keep.tile([P, entries // LIST_ROWS], U16, name=name)
            nc.sync.dma_start(lst[:], src)
            return lst

        def load_scale_rows(queue, dst, src):
            for q in range(4):
                queue.dma_start(
                    dst[32 * q : 32 * q + 4, :, :].bitcast(I32),
                    src[:, 4 * q : 4 * q + 4, :].rearrange("a r n -> r a n").bitcast(I32),
                )

        def load_weight_block(w, a, b):
            block = raw.tile([P, PACK, PASS], F32, name="w_raw", tag="w_raw")
            rows = w[a * PASS : (a + 1) * PASS, b * PASS : (b + 1) * PASS]
            nc.sync.dma_start(block[:], rows.rearrange("(p j) c -> p j c", j=PACK))
            return block

        def round_weight_block(block):
            rounded = work.tile([P, PASS * PACK], BF16, name="w_bf16", align_bytes=64)
            nc.scalar.activation(
                out=rounded[:].rearrange("p (t m j) -> p m t j", t=PACK, j=PACK),
                in_=block[:].rearrange("p j (m t) -> p m t j", t=PACK),
                func=ACT.Copy,
            )
            return rounded

        def quantise(name, rounded):
            codes = keep.tile([P, PASS], U32, name=name + "_codes", align_bytes=64)
            scales = keep.tile([P, PASS], U8, name=name + "_scales", align_bytes=64)
            nc.vector.quantize_mx(out=codes[:].bitcast(FP8X4), scales=scales[:], in_=rounded[:])
            return codes, scales

        table_scales = keep.tile([P, T], U8, name="table_scales")
        nc.vector.memset(table_scales[:].bitcast(I32), 0)
        v_scales = [keep.tile([P, S], U8, name="v_scales%d" % a, align_bytes=64) for a in range(passes)]
        nc.gpsimd.memset(v_scales[1][:].bitcast(I32), 0)
        w2_scale_rows = keep.tile([P, passes, H], U8, name="w2_scale_rows")
        nc.gpsimd.memset(w2_scale_rows[:].rearrange("p a n -> p (a n)").bitcast(I32), 0)

        entry_list = load_list("entry_list", offs, S)
        side_lists = [load_list("side1_list", pos1, C), load_list("side2_list", pos2, C)]
        contact_list = load_list("contact_list", pos3, S)
        row_scale = keep.tile([P, groups, PACK], F32, name="row_scale")
        nc.sync.dma_start(row_scale[:], hs.rearrange("(b p t) -> p b t", b=groups, t=PACK))
        w2_raw = keep.tile([P, passes, 2 * H], U8, name="w2_raw")
        for a in range(passes):
            nc.sync.dma_start(w2_raw[:, a, :].bitcast(I32), w2_words[a].bitcast(I32))
        w1_raw = {(0, 0): load_weight_block(w1, 0, 0)}
        for q in range(4):
            nc.sync.dma_start(
                table_scales[32 * q : 32 * q + 8, :].bitcast(I32), tab_scales[:, 4 * q : 4 * q + 4, :].bitcast(I32)
            )
        load_scale_rows(nc.sync, w2_scale_rows, w2_scales)

        def load_table(a):
            words = wide.tile([P, T], I32, name="table_words", tag="wide")
            nc.sync.dma_start(words[:], tab_words[a].rearrange("p n i -> p (n i)").bitcast(I32))
            return words

        w1_raw[1, 0] = load_weight_block(w1, 1, 0)
        table = [load_table(a) for a in range(passes)]

        w2_codes = keep.tile([P, passes * groups, PACK, 2 * P], U8, name="w2_codes", align_bytes=64)
        nc.vector.tensor_copy(
            w2_codes[:].bitcast(U16),
            w2_raw[:].bitcast(U16).rearrange("p a (b m t) -> p (a b) t m", b=groups, t=PACK),
        )

        v_codes = keep.tile([P, passes, S], U32, name="v_codes", align_bytes=64)
        nc.vector.tensor_copy(v_scales[0][:], table_scales[:].indirect(entry_list[:]))
        nc.sync.dma_start(v_scales[1][0:112, :].bitcast(I32), v_scales[0][4:116, :].bitcast(I32))
        w2_planes = keep.tile([P, passes * groups, PACK, P], U8, name="w2_planes", align_bytes=64)
        nc.vector.tensor_copy(
            w2_planes[:], w2_scale_rows[:].rearrange("p a (b m t) -> p (a b) t m", b=groups, t=PACK)
        )
        w1_mx = {}
        for a in range(passes):
            w1_mx[a, 0] = quantise("w1_%d0" % a, round_weight_block(w1_raw[a, 0]))
        nc.vector.tensor_copy(v_codes[:, 0, :], table[0][:].bitcast(U32).indirect(entry_list[:]))
        cols = BANK // LIST_ROWS
        for u in range(S // BANK):
            nc.vector.tensor_copy(
                v_codes[:, 1, u * BANK : (u + 1) * BANK],
                table[1][:].bitcast(U32).indirect(entry_list[:, u * cols : (u + 1) * cols]),
            )

        h = [keep.tile([P, S], F32, name="h%d" % i) for i in range(len(row_tiles))]
        picked = {}
        low_mx = {}
        w3_mx = {}

        def products(i, u):
            b, t = row_tiles[i]
            entries = slice(u * BANK, (u + 1) * BANK)
            rows = slice(t * P, (t + 1) * P)
            first = psum.tile([P, BANK], F32, name="acc", tag="acc")
            for a in range(passes):
                codes, scales = w1_mx[a, b]
                nc.tensor.matmul_mx(
                    out=first[:], lhsT=codes[:, rows].bitcast(FP8X4), lhsT_scale=scales[:, rows],
                    rhs=v_codes[:, a, entries].bitcast(FP8X4), rhs_scale=v_scales[a][:, entries],
                    start=(a == 0), stop=(a == passes - 1),
                )
            second = psum.tile([P, BANK], F32, name="acc", tag="acc")
            for a in range(passes):
                nc.tensor.matmul_mx(
                    out=second[:], lhsT=w2_codes[:, a * groups + b, t, :].bitcast(FP4X4),
                    lhsT_scale=w2_planes[:, a * groups + b, t, :],
                    rhs=v_codes[:, a, entries].bitcast(FP8X4), rhs_scale=v_scales[a][:, entries],
                    start=(a == 0), stop=(a == passes - 1),
                )
            if i == 0:
                squared = work.tile([P, BANK], F32, name="squared", bufs=2)[:]
            else:
                squared = picked_slice(i - 1, u)
            nc.scalar.activation(out=squared, in_=first[:], func=ACT.Square)
            cubic = work.tile([P, BANK], F32, name="cubic")
            nc.vector.tensor_tensor(cubic[:], second[:], squared, ALU.mult)
            if i < NV:
                nc.vector.tensor_tensor(h[i][:, entries], cubic[:], first[:], ALU.subtract)
            else:
                linear = work.tile([P, BANK], F32, name="linear")
                nc.scalar.copy(linear[:], first[:])
                nc.gpsimd.tensor_tensor(h[i][:, entries], cubic[:], linear[:], ALU.subtract)

        def picked_slice(i, side):
            b, t = row_tiles[i]
            if b not in picked:
                picked[b] = wide.tile([P, 2, PACK, C], F32, name="picked", tag="wide")
            return picked[b][:, side, t, :]

        def pick_side(i, side):
            nc.vector.tensor_copy(picked_slice(i, side), h[i][:].indirect(side_lists[side][:]))

        def smaller_side(b):
            low = work.tile([P, C * PACK], BF16, name="low", tag="low", align_bytes=64, bufs=1)
            nc.vector.tensor_tensor(
                low[:].rearrange("p (c i t) -> p c t i", i=4, t=PACK),
                picked[b][:, 0, :, :].rearrange("p t (c i) -> p c t i", i=4),
                picked[b][:, 1, :, :].rearrange("p t (c i) -> p c t i", i=4),
                ALU.min,
            )
            return low

        later_blocks = [("w1", a, 1) for a in range(passes)] + [("w3", a, b) for b in range(groups) for a in range(groups)]
        pending = None
        late = []
        for i in range(len(row_tiles)):
            for u in range(S // BANK):
                products(i, u)
                if i > 0:
                    pick_side(i - 1, u)
            if pending is not None:
                name, a, b, rounded = pending
                (w1_mx if name == "w1" else w3_mx)[a, b] = quantise("%s_%d%d" % (name, a, b), rounded)
                pending = None
            if i in CASTS:
                name, a, b = later_blocks[CASTS.index(i)]
                block = load_weight_block(w1 if name == "w1" else w3, a, b)
                if LATE and name == "w3" and b == 1:
                    late.append((a, round_weight_block(block)))
                else:
                    pending = (name, a, b, round_weight_block(block))
            if i == PACK:
                low_first = smaller_side(0)
            if i == PACK + 1:
                low_mx[0] = quantise("low0", low_first)
        last = len(row_tiles) - 1
        pick_side(last, 0)
        pick_side(last, 1)
        if pending is not None:
            name, a, b, rounded = pending
            w3_mx[a, b] = quantise("%s_%d%d" % (name, a, b), rounded)
        low_mx[1] = quantise("low1", smaller_side(1))
        if LATE:
            late_codes = work.tile([P, groups, PASS], U32, name="late_codes", tag="low", align_bytes=64, bufs=1)
            for a, rounded in late:
                scales = keep.tile([P, PASS], U8, name="late_scales%d" % a, align_bytes=64)
                nc.vector.quantize_mx(out=late_codes[:, a, :].bitcast(FP8X4), scales=scales[:], in_=rounded[:])
                w3_mx[a, 1] = (late_codes[:, a, :], scales)
        for i in HS:
            b, t = row_tiles[i]
            nc.scalar.activation(out=h[i][:], in_=h[i][:], func=ACT.Copy, scale=row_scale[:, b, t : t + 1])
        for i in HG:
            b, t = row_tiles[i]
            nc.gpsimd.tensor_scalar(h[i][:], h[i][:], row_scale[:, b, t : t + 1], 0.0, ALU.mult, ALU.add)

        y = [keep.tile([P, C + SPARE], F32, name="y%d" % r) for r in range(RING)]
        for r in range(RING):
            nc.gpsimd.memset(y[r][:, C:], 0.0)

        def second_stage(i):
            b, t = row_tiles[i]
            rows = slice(t * P, (t + 1) * P)
            acc = psum.tile([P, C], F32, name="acc", tag="acc")
            for a in range(groups):
                codes, scales = w3_mx[a, b]
                nc.tensor.matmul_mx(
                    out=acc[:], lhsT=codes[:, rows].bitcast(FP8X4), lhsT_scale=scales[:, rows],
                    rhs=low_mx[a][0][:].bitcast(FP8X4), rhs_scale=low_mx[a][1][:],
                    start=(a == 0), stop=(a == groups - 1),
                )
            if i in EV:
                nc.vector.tensor_copy(y[i % RING][:, :C], acc[:])
            else:
                nc.scalar.copy(y[i % RING][:, :C], acc[:])

        fetched_groups = {}

        def fetched_slice(i, lo, hi):
            b, t = row_tiles[i]
            if b not in fetched_groups:
                fetched_groups[b] = wide.tile([P, PACK, S], F32, name="fetched", tag="wide")
            return fetched_groups[b][:, t, lo:hi]

        def fetch(i):
            for lo in range(0, S, GP[i]):
                hi = lo + GP[i]
                nc.vector.tensor_copy(
                    fetched_slice(i, lo, hi),
                    y[i % RING][:].indirect(contact_list[:, lo // LIST_ROWS : hi // LIST_ROWS]),
                )

        def damp(i, lo, hi):
            fetched = fetched_slice(i, lo, hi)
            magnitude = work.tile([P, hi - lo], F32, name="magnitude", bufs=MB)
            nc.scalar.activation(out=magnitude[:], in_=fetched, func=ACT.Abs)
            nc.scalar.activation(out=fetched, in_=magnitude[:], func=ACT.Exp, scale=-1.0)
            return fetched

        out_rows = out.rearrange("(b p t) j -> b t p j", b=groups, t=PACK)

        def finish(i, lo, hi, damping):
            b, t = row_tiles[i]
            if i in FV:
                nc.vector.scalar_tensor_tensor(
                    out=h[i][:, lo:hi], in0=h[i][:, lo:hi], scalar=row_scale[:, b, t : t + 1], in1=damping,
                    op0=ALU.mult, op1=ALU.mult,
                )
            else:
                if i not in HS and i not in HG:
                    nc.gpsimd.tensor_scalar(damping, damping, row_scale[:, b, t : t + 1], 0.0, ALU.mult, ALU.add)
                nc.gpsimd.tensor_tensor(h[i][:, lo:hi], h[i][:, lo:hi], damping, ALU.mult)
            nc.sync.dma_start(out_rows[b, t][:, lo:hi], h[i][:, lo:hi])

        for i in range(RING):
            second_stage(i)
        waiting = []
        for i in range(len(row_tiles)):
            fetch(i)
            if i + RING <= last:
                second_stage(i + RING)
            lo = 0
            for width in SP[i]:
                waiting.append((i, lo, lo + width, damp(i, lo, lo + width)))
                lo = lo + width
            while len(waiting) > 0 and waiting[0][0] < i:
                finish(*waiting[0])
                waiting = waiting[1:]
        for step in waiting:
            finish(*step)
